import numpy as np
import ml_dtypes


def mxq(x, axis, fmt="e4m3"):
    dtype, down = {"e4m3": (ml_dtypes.float8_e4m3fn, 7), "e5m2": (ml_dtypes.float8_e5m2, 14)}[fmt]
    v = np.moveaxis(np.asarray(x, np.float32).astype(ml_dtypes.bfloat16).astype(np.float64), axis, -1)
    blocks = v.reshape(v.shape[:-1] + (-1, 32))
    amax = np.abs(blocks).max(-1, keepdims=True)
    byte = np.maximum(np.where(amax > 0, np.frexp(amax)[1] - 1 + 127, 0) - down, 1)
    scale = np.exp2(byte - 127.0)
    codes = (blocks / scale).astype(np.float32).astype(dtype).astype(np.float64)
    return np.moveaxis((codes * scale).reshape(v.shape), -1, axis)


WIDE = False


def mx_kscale(k):
    if not WIDE:
        return np.ones(k)
    levels = np.array([30, -30])
    if k % 512:
        return np.exp2(np.random.permutation(np.resize(levels, k // 32))).repeat(32)
    a = np.empty((k // 512, 16))
    for p in range(k // 512):
        a[p, :8] = np.random.permutation(np.resize(levels, 8))
        for g in range(8):
            far = levels[np.abs(levels - a[p, g]) >= 10]
            a[p, g + 8] = far[np.random.randint(len(far))]
    return np.exp2(a.ravel()).repeat(32)


def f64(x):
    return np.asarray(x).astype(np.float64)


def striped(idx):
    return np.tile(np.asarray(idx).reshape(-1, 16).T, (8, 1)).astype(np.uint16)


def unstriped(offs):
    return offs[:16].T.reshape(-1).astype(np.int64)


E2M1 = np.array([0.0, 0.5, 1.0, 1.5, 2.0, 3.0, 4.0, 6.0, -0.0, -0.5, -1.0, -1.5, -2.0, -3.0, -4.0, -6.0])


def pack_weight(w, fmt):
    k, n = w.shape
    w = f64(np.asarray(w, np.float32).astype(ml_dtypes.bfloat16)).reshape(k // 32, 32, n)
    amax = np.abs(w).max(1)
    if fmt in ("e4m3", "e5m2"):
        byte = np.frexp(amax)[1] - 1 + 127 - (7 if fmt == "e4m3" else 14)
    else:
        mant, ex = np.frexp(amax / 6.0)
        byte = np.where(mant > 0.5, ex, ex - 1) + 127
    byte = np.clip(np.where(amax > 0, byte, 1), 1, 254)
    scaled = (w * np.exp2(127.0 - byte)[:, None, :]).reshape(k, n).astype(np.float32)
    by_word = np.ascontiguousarray(scaled.reshape(k // 512, 128, 4, n).transpose(0, 1, 3, 2))
    if fmt in ("e4m3", "e5m2"):
        words = by_word.astype(ml_dtypes.float8_e4m3fn if fmt == "e4m3" else ml_dtypes.float8_e5m2).view(np.uint8)
    else:
        c = by_word.astype(ml_dtypes.float4_e2m1fn).view(np.uint8) & 0xF
        words = (c[..., 0::2] | (c[..., 1::2] << 4)).reshape(k // 512, 128, 2 * n)
    return np.ascontiguousarray(words), np.ascontiguousarray(byte.astype(np.uint8).reshape(k // 512, 16, n))


def unpack_weight(words, scales, fmt):
    g, _, n = scales.shape
    words = np.ascontiguousarray(words).reshape(g, 128, n, -1)
    if fmt in ("e4m3", "e5m2"):
        vals = words.view(ml_dtypes.float8_e4m3fn if fmt == "e4m3" else ml_dtypes.float8_e5m2).astype(np.float64)
    else:
        nib = np.empty((g, 128, n, 4), np.uint8)
        nib[..., 0::2] = words & 0xF
        nib[..., 1::2] = words >> 4
        vals = E2M1[nib]
    vals = vals * np.repeat(np.exp2(scales.astype(np.float64) - 127.0), 8, axis=1)[..., None]
    return vals.transpose(0, 1, 3, 2).reshape(g * 512, n)


def sigmoid(v):
    return 1.0 / (1.0 + np.exp(-v))


K, T, J, R, O, N, L = 512, 1024, 256, 512, 128, 256, 512


def setup_inputs():
    n = np.random.standard_normal
    idx = np.random.permutation(T)[:J]
    idx2 = np.random.permutation(J)[:O]
    idx3 = np.random.permutation(J)[:O]
    fk = mx_kscale(K)
    fr = mx_kscale(R)
    fl = mx_kscale(L)
    xtp = pack_weight(n((K, T)) / fk[:, None], "e5m2")
    wp = pack_weight(n((K, R)) * 1 / np.sqrt(K) * fk[:, None], "e2m1")
    w2p = pack_weight(n((K, R)) * 1 / np.sqrt(K) * fk[:, None] * fr, "e4m3")
    wbp = pack_weight(n((R, N)) * 1 / np.sqrt(R) / fr[:, None], "e2m1")
    sxp = pack_weight(n((L, O)) / fl[:, None], "e4m3")
    wsp = pack_weight(n((L, N)) * 1 / np.sqrt(L) * fl[:, None], "e2m1")
    return {
        "xt_words": xtp[0],
        "xt_scales": xtp[1],
        "w_words": wp[0],
        "w_scales": wp[1],
        "w2_words": w2p[0],
        "w2_scales": w2p[1],
        "sg": (np.random.uniform(0.6, 1.6, (R, 1))).astype(np.float32),
        "wb_words": wbp[0],
        "wb_scales": wbp[1],
        "sx_words": sxp[0],
        "sx_scales": sxp[1],
        "ws_words": wsp[0],
        "ws_scales": wsp[1],
        "offs": striped(idx),
        "offs2": striped(idx2),
        "offs3": striped(idx3),
    }


def reference(xt_words, xt_scales, w_words, w_scales, w2_words, w2_scales, sg, wb_words, wb_scales, sx_words, sx_scales, ws_words, ws_scales, offs, offs2, offs3):
    idx = unstriped(offs)
    idx2 = unstriped(offs2)
    idx3 = unstriped(offs3)
    xtu = unpack_weight(xt_words, xt_scales, "e5m2")
    wu = unpack_weight(w_words, w_scales, "e2m1")
    w2u = unpack_weight(w2_words, w2_scales, "e4m3")
    wbu = unpack_weight(wb_words, wb_scales, "e2m1")
    sxu = unpack_weight(sx_words, sx_scales, "e4m3")
    wsu = unpack_weight(ws_words, ws_scales, "e2m1")
    xtidxg = xtu[:, idx]
    a = wu.T @ xtidxg
    b = w2u.T @ xtidxg
    hid = np.maximum(b[:, idx2], b[:, idx3]) * sigmoid(a[:, idx3] * f64(sg))
    hidq = mxq(hid, 0, "e4m3")
    y = wbu.T @ hidq + wsu.T @ sxu
    return y

@@ -1,0 +1,173 @@
+from contextlib import ExitStack
+
+import concourse.mybir as mybir
+
+K, T, J, R, O, N, L = 512, 1024, 256, 512, 128, 256, 512
+FLOPS = 2 * (2 * K * R * J + R * N * O + L * N * O)
+
+F32 = mybir.dt.float32
+BF16 = mybir.dt.bfloat16
+I32 = mybir.dt.int32
+U32 = mybir.dt.uint32
+U16 = mybir.dt.uint16
+U8 = mybir.dt.uint8
+E4M3 = mybir.dt.float8_e4m3fn_x4
+E5M2 = mybir.dt.float8_e5m2_x4
+E2M1 = mybir.dt.float4_e2m1fn_x4
+ACT = mybir.ActivationFunctionType
+ALU = mybir.AluOpType
+
+P = 128
+PACK = 4
+ROWS = 16
+QUAD = 32
+TOP = P - ROWS
+
+
+def tile_list_twow_agree_skip_plain_kernel(
+    tc, xt_words, xt_scales, w_words, w_scales, w2_words, w2_scales, sg,
+    wb_words, wb_scales, sx_words, sx_scales, ws_words, ws_scales, offs, offs2, offs3, out,
+):
+    nc = tc.nc
+    with ExitStack() as ctx:
+        sb = ctx.enter_context(tc.tile_pool(name="sb", bufs=1))
+        psum = ctx.enter_context(tc.psum_pool(name="psum", bufs=8))
+
+        def tile(name, cols, dtype):
+            return sb.tile([P, cols], dtype, name=name, align_bytes=64)
+
+        idx = tile("idx", J // 16, U16)
+        idx2 = tile("idx2", O // 16, U16)
+        idx3 = tile("idx3", O // 16, U16)
+        xt = tile("xt", T, U32)
+        xt_rows = tile("xt_rows", T, U8)
+        w_rows = tile("w_rows", 2 * R, U8)
+        rows = tile("rows", 2 * R, U8)
+        planes = tile("planes", 2 * R, U8)
+        xg_plane = tile("xg_plane", J, U8)
+        w_raw = tile("w_raw", 2 * R, U8)
+        w2_raw = tile("w2_raw", R, U32)
+        w_dealt = tile("w_dealt", 2 * R, U8)
+        w2_dealt = tile("w2_dealt", R, U32)
+        xg = tile("xg", J, U32)
+        xg_rows = tile("xg_rows", J, U8)
+        slope = tile("slope", PACK, F32)
+
+        nc.vector.memset(xt_rows[0:TOP, :].bitcast(I32), 0)
+        nc.vector.memset(w_rows[0:TOP, :].bitcast(I32), 0)
+        nc.vector.memset(planes[:].bitcast(I32), 0)
+        nc.vector.memset(xg_plane[:].bitcast(I32), 0)
+
+        nc.sync.dma_start(idx[:], offs)
+        nc.sync.dma_start(xt[:].bitcast(I32), xt_words[0].rearrange("p n t -> p (n t)").bitcast(I32))
+        nc.scalar.dma_start(xt_rows[TOP:P, :].bitcast(I32), xt_scales[0].bitcast(I32))
+        nc.scalar.dma_start(w_rows[TOP:P, R : 2 * R].bitcast(I32), w2_scales[0].bitcast(I32))
+        nc.scalar.dma_start(w_rows[TOP:P, 0:R].bitcast(I32), w_scales[0].bitcast(I32))
+        nc.sync.dma_start(w2_raw[:].bitcast(I32), w2_words[0].rearrange("p n t -> p (n t)").bitcast(I32))
+        nc.sync.dma_start(w_raw[:].bitcast(I32), w_words[0].bitcast(I32))
+        nc.sync.dma_start(idx3[:], offs3)
+        nc.sync.dma_start(idx2[:], offs2)
+        warm_in = tile("warm_in", 1, F32)
+        warm_out = tile("warm_out", 1, F32)
+        nc.vector.memset(warm_in[:], 0.0)
+        nc.scalar.activation(warm_out[:], warm_in[:], ACT.Sigmoid)
+        nc.gpsimd.dma_start(slope[:], sg.rearrange("(p t) o -> p (t o)", t=PACK))
+
+        def spread(plane, source):
+            for q in range(4):
+                queue = nc.sync if q % 2 == 0 else nc.scalar
+                queue.dma_start(
+                    plane[QUAD * q : QUAD * q + 4, :].bitcast(I32),
+                    source[TOP + 4 * q : TOP + 4 * q + 4, :].bitcast(I32),
+                )
+
+        nc.vector.tensor_copy(xg_rows[:], xt_rows[:].indirect(idx[:]))
+        spread(xg_plane, xg_rows)
+        nc.vector.tensor_copy(
+            rows[:, 0 : 2 * R].rearrange("p (g t m) -> p g t m", g=2, t=PACK),
+            w_rows[:].rearrange("p (g m t) -> p g t m", g=2, t=PACK),
+        )
+        spread(planes, rows)
+        nc.vector.tensor_copy(xg[:], xt[:].indirect(idx[:]))
+        nc.vector.tensor_copy(
+            w2_dealt[:].rearrange("p (t c i) -> p c t i", t=PACK, i=4),
+            w2_raw[:].rearrange("p (c i t) -> p c t i", t=PACK, i=4),
+        )
+        nc.scalar.copy(
+            w_dealt[:].bitcast(U16).rearrange("p (t c i) -> p c t i", t=PACK, i=8),
+            w_raw[:].bitcast(U16).rearrange("p (c i t) -> p c t i", t=PACK, i=8),
+        )
+
+        wb = w_raw[:, 0 : 2 * N]
+        ws = w_raw[:, 2 * N : 4 * N]
+        sx = w2_raw[:, 0:O]
+        wb_plane = rows[:, 0:N]
+        ws_plane = rows[:, N : 2 * N]
+        sx_plane = rows[:, 2 * N : 2 * N + O]
+        nc.sync.dma_start(sx.bitcast(I32), sx_words[0].rearrange("p n t -> p (n t)").bitcast(I32))
+        nc.sync.dma_start(ws.bitcast(I32), ws_words[0].bitcast(I32))
+        nc.sync.dma_start(wb.bitcast(I32), wb_words[0].bitcast(I32))
+        for plane, scales in ((sx_plane, sx_scales), (ws_plane, ws_scales), (wb_plane, wb_scales)):
+            for r in range(4):
+                nc.sync.dma_start(plane[r:P:QUAD, :].bitcast(I32), scales[0][r:ROWS:4, :].bitcast(I32))
+
+        top = tile("top", PACK * O, F32)
+        gate = tile("gate", PACK * O, F32)
+        for t in range(PACK):
+            cols = slice(t * P, (t + 1) * P)
+            b_ps = psum.tile([P, J], F32, name="acc")
+            nc.tensor.matmul_mx(
+                b_ps[:], lhsT=w2_dealt[:, cols].bitcast(E4M3), lhsT_scale=planes[:, R + t * P : R + (t + 1) * P],
+                rhs=xg[:].bitcast(E5M2), rhs_scale=xg_plane[:], start=True, stop=True,
+            )
+            a_ps = psum.tile([P, J], F32, name="acc")
+            nc.tensor.matmul_mx(
+                a_ps[:], lhsT=w_dealt[:, 2 * t * P : 2 * (t + 1) * P].bitcast(E2M1), lhsT_scale=planes[:, cols],
+                rhs=xg[:].bitcast(E5M2), rhs_scale=xg_plane[:], start=True, stop=True,
+            )
+            a = tile("a%d" % t, J, F32)
+            b = tile("b%d" % t, J, F32)
+            if t == 0:
+                nc.vector.tensor_copy(b[:], b_ps[:])
+            else:
+                nc.scalar.copy(b[:], b_ps[:])
+            nc.scalar.copy(a[:], a_ps[:])
+            nc.scalar.activation(
+                gate[:, cols], a[:].indirect(idx3[:]), ACT.Sigmoid, scale=slope[:, t : t + 1]
+            )
+            b2 = tile("b2_%d" % t, O, F32)
+            b3 = tile("b3_%d" % t, O, F32)
+            nc.vector.tensor_copy(b2[:], b[:].indirect(idx2[:]))
+            nc.vector.tensor_copy(b3[:], b[:].indirect(idx3[:]))
+            nc.vector.tensor_tensor(top[:, cols], b2[:], b3[:], ALU.max)
+
+        hid = tile("hid", PACK * O, BF16)
+        nc.vector.tensor_tensor(
+            hid[:].rearrange("p (c i t) -> p c t i", t=PACK, i=4),
+            top[:].rearrange("p (t c i) -> p c t i", t=PACK, i=4),
+            gate[:].rearrange("p (t c i) -> p c t i", t=PACK, i=4),
+            ALU.mult,
+        )
+        hq = tile("hq", O, U32)
+        hq_plane = tile("hq_plane", O, U8)
+        nc.vector.quantize_mx(hq[:].bitcast(E4M3), hq_plane[:], hid[:])
+
+        for h in range(N // P):
+            y_ps = psum.tile([P, J], F32, name="acc")
+            words = slice(2 * h * P, 2 * (h + 1) * P)
+            cols = slice(h * P, (h + 1) * P)
+            nc.tensor.matmul_mx(
+                y_ps[:, 0:O], lhsT=ws[:, words].bitcast(E2M1), lhsT_scale=ws_plane[:, cols],
+                rhs=sx.bitcast(E4M3), rhs_scale=sx_plane, start=True, stop=False,
+            )
+            nc.tensor.matmul_mx(
+                y_ps[:, 0:O], lhsT=wb[:, words].bitcast(E2M1), lhsT_scale=wb_plane[:, cols],
+                rhs=hq[:].bitcast(E4M3), rhs_scale=hq_plane[:], start=False, stop=True,
+            )
+            y = tile("y%d" % h, O, F32)
+            if h == 0:
+                nc.vector.tensor_copy(y[:], y_ps[:, 0:O])
+                nc.sync.dma_start(out[cols, :], y[:])
+            else:
+                nc.scalar.copy(y[:], y_ps[:, 0:O])
+                nc.scalar.dma_start(out[cols, :], y[:])

@@ -31,7 +31,7 @@ def tile_list_twow_agree_skip_plain_kernel(
     nc = tc.nc
     with ExitStack() as ctx:
         sb = ctx.enter_context(tc.tile_pool(name="sb", bufs=1))
-        psum = ctx.enter_context(tc.psum_pool(name="psum", bufs=8))
+        psum = ctx.enter_context(tc.psum_pool(name="psum", bufs=1))
 
         def tile(name, cols, dtype):
             return sb.tile([P, cols], dtype, name=name, align_bytes=64)
@@ -41,10 +41,11 @@ def tile_list_twow_agree_skip_plain_kernel(
         idx3 = tile("idx3", O // 16, U16)
         xt = tile("xt", T, U32)
         xt_rows = tile("xt_rows", T, U8)
-        w_rows = tile("w_rows", 2 * R, U8)
-        rows = tile("rows", 2 * R, U8)
-        planes = tile("planes", 2 * R, U8)
-        xg_plane = tile("xg_plane", J, U8)
+        w2_rows = tile("w2_rows", R, U8)
+        w_plane = tile("w_plane", R, U8)
+        rows = tile("rows", 2 * R + J, U8)
+        planes = tile("planes", 2 * R + J, U8)
+        xg_plane = planes[:, 2 * R :]
         w_raw = tile("w_raw", 2 * R, U8)
         w2_raw = tile("w2_raw", R, U32)
         w_dealt = tile("w_dealt", 2 * R, U8)
@@ -54,18 +55,17 @@ def tile_list_twow_agree_skip_plain_kernel(
         slope = tile("slope", PACK, F32)
 
         nc.vector.memset(xt_rows[0:TOP, :].bitcast(I32), 0)
-        nc.vector.memset(w_rows[0:TOP, :].bitcast(I32), 0)
+        nc.vector.memset(w2_rows[0:TOP, :].bitcast(I32), 0)
         nc.vector.memset(planes[:].bitcast(I32), 0)
-        nc.vector.memset(xg_plane[:].bitcast(I32), 0)
 
         nc.sync.dma_start(idx[:], offs)
-        nc.sync.dma_start(xt[:].bitcast(I32), xt_words[0].rearrange("p n t -> p (n t)").bitcast(I32))
         nc.scalar.dma_start(xt_rows[TOP:P, :].bitcast(I32), xt_scales[0].bitcast(I32))
-        nc.scalar.dma_start(w_rows[TOP:P, R : 2 * R].bitcast(I32), w2_scales[0].bitcast(I32))
-        nc.scalar.dma_start(w_rows[TOP:P, 0:R].bitcast(I32), w_scales[0].bitcast(I32))
+        nc.sync.dma_start(w2_rows[TOP:P, :].bitcast(I32), w2_scales[0].bitcast(I32))
+        nc.scalar.dma_start(rows[TOP:P, 0:R].bitcast(I32), w_scales[0].bitcast(I32))
+        nc.sync.dma_start(idx3[:], offs3)
+        nc.sync.dma_start(xt[:].bitcast(I32), xt_words[0].rearrange("p n t -> p (n t)").bitcast(I32))
         nc.sync.dma_start(w2_raw[:].bitcast(I32), w2_words[0].rearrange("p n t -> p (n t)").bitcast(I32))
         nc.sync.dma_start(w_raw[:].bitcast(I32), w_words[0].bitcast(I32))
-        nc.sync.dma_start(idx3[:], offs3)
         nc.sync.dma_start(idx2[:], offs2)
         warm_in = tile("warm_in", 1, F32)
         warm_out = tile("warm_out", 1, F32)
@@ -82,11 +82,10 @@ def tile_list_twow_agree_skip_plain_kernel(
                 )
 
         nc.vector.tensor_copy(xg_rows[:], xt_rows[:].indirect(idx[:]))
-        spread(xg_plane, xg_rows)
         nc.vector.tensor_copy(
-            rows[:, 0 : 2 * R].rearrange("p (g t m) -> p g t m", g=2, t=PACK),
-            w_rows[:].rearrange("p (g m t) -> p g t m", g=2, t=PACK),
+            rows[:, R : 2 * R].rearrange("p (t m) -> p t m", t=PACK), w2_rows[:].rearrange("p (m t) -> p t m", t=PACK)
         )
+        nc.vector.tensor_copy(rows[:, 2 * R :].bitcast(I32), xg_rows[:].bitcast(I32))
         spread(planes, rows)
         nc.vector.tensor_copy(xg[:], xt[:].indirect(idx[:]))
         nc.vector.tensor_copy(
@@ -98,12 +97,16 @@ def tile_list_twow_agree_skip_plain_kernel(
             w_raw[:].bitcast(U16).rearrange("p (c i t) -> p c t i", t=PACK, i=8),
         )
 
+        nc.vector.tensor_copy(
+            w_plane[:].rearrange("p (t m) -> p t m", t=PACK), planes[:, 0:R].rearrange("p (m t) -> p t m", t=PACK)
+        )
         wb = w_raw[:, 0 : 2 * N]
         ws = w_raw[:, 2 * N : 4 * N]
         sx = w2_raw[:, 0:O]
-        wb_plane = rows[:, 0:N]
-        ws_plane = rows[:, N : 2 * N]
-        sx_plane = rows[:, 2 * N : 2 * N + O]
+        spare = w2_raw[:, O:R].bitcast(U8)
+        wb_plane = spare[:, 0:N]
+        ws_plane = spare[:, N : 2 * N]
+        sx_plane = spare[:, 2 * N : 2 * N + O]
         nc.sync.dma_start(sx.bitcast(I32), sx_words[0].rearrange("p n t -> p (n t)").bitcast(I32))
         nc.sync.dma_start(ws.bitcast(I32), ws_words[0].bitcast(I32))
         nc.sync.dma_start(wb.bitcast(I32), wb_words[0].bitcast(I32))
@@ -113,61 +116,96 @@ def tile_list_twow_agree_skip_plain_kernel(
 
         top = tile("top", PACK * O, F32)
         gate = tile("gate", PACK * O, F32)
-        for t in range(PACK):
-            cols = slice(t * P, (t + 1) * P)
-            b_ps = psum.tile([P, J], F32, name="acc")
+        a = [tile("a%d" % t, J, F32) for t in range(PACK)]
+        b = [tile("b%d" % t, J, F32) for t in range(PACK)]
+        b2 = tile("by2", PACK * O, F32)
+        b3 = tile("by3", PACK * O, F32)
+
+        def cols(t):
+            return slice(t * P, (t + 1) * P)
+
+        def product_a(t):
+            acc = psum.tile([P, J], F32, name="bank_a%d" % t)
             nc.tensor.matmul_mx(
-                b_ps[:], lhsT=w2_dealt[:, cols].bitcast(E4M3), lhsT_scale=planes[:, R + t * P : R + (t + 1) * P],
-                rhs=xg[:].bitcast(E5M2), rhs_scale=xg_plane[:], start=True, stop=True,
+                acc[:], lhsT=w_dealt[:, 2 * t * P : 2 * (t + 1) * P].bitcast(E2M1), lhsT_scale=w_plane[:, cols(t)],
+                rhs=xg[:].bitcast(E5M2), rhs_scale=xg_plane, start=True, stop=True,
             )
-            a_ps = psum.tile([P, J], F32, name="acc")
+            nc.scalar.copy(a[t][:], acc[:])
+
+        def product_b(t):
+            acc = psum.tile([P, J], F32, name="bank_b%d" % t)
             nc.tensor.matmul_mx(
-                a_ps[:], lhsT=w_dealt[:, 2 * t * P : 2 * (t + 1) * P].bitcast(E2M1), lhsT_scale=planes[:, cols],
-                rhs=xg[:].bitcast(E5M2), rhs_scale=xg_plane[:], start=True, stop=True,
+                acc[:], lhsT=w2_dealt[:, cols(t)].bitcast(E4M3), lhsT_scale=planes[:, R + t * P : R + (t + 1) * P],
+                rhs=xg[:].bitcast(E5M2), rhs_scale=xg_plane, start=True, stop=True,
             )
-            a = tile("a%d" % t, J, F32)
-            b = tile("b%d" % t, J, F32)
             if t == 0:
-                nc.vector.tensor_copy(b[:], b_ps[:])
+                nc.vector.tensor_copy(b[t][:], acc[:])
             else:
-                nc.scalar.copy(b[:], b_ps[:])
-            nc.scalar.copy(a[:], a_ps[:])
-            nc.scalar.activation(
-                gate[:, cols], a[:].indirect(idx3[:]), ACT.Sigmoid, scale=slope[:, t : t + 1]
-            )
-            b2 = tile("b2_%d" % t, O, F32)
-            b3 = tile("b3_%d" % t, O, F32)
-            nc.vector.tensor_copy(b2[:], b[:].indirect(idx2[:]))
-            nc.vector.tensor_copy(b3[:], b[:].indirect(idx3[:]))
-            nc.vector.tensor_tensor(top[:, cols], b2[:], b3[:], ALU.max)
+                nc.scalar.copy(b[t][:], acc[:])
+
+        def look(t):
+            nc.scalar.activation(gate[:, cols(t)], a[t][:].indirect(idx3[:]), ACT.Sigmoid, scale=slope[:, t : t + 1])
+
+        def pick(t):
+            nc.vector.tensor_copy(b2[:, cols(t)], b[t][:].indirect(idx2[:]))
+            nc.vector.tensor_copy(b3[:, cols(t)], b[t][:].indirect(idx3[:]))
+
+        def larger(t):
+            nc.vector.tensor_tensor(top[:, cols(t)], b2[:, cols(t)], b3[:, cols(t)], ALU.max)
+
+        product_b(0)
+        product_b(1)
+        pick(0)
+        product_a(0)
+        product_b(2)
+        pick(1)
+        larger(0)
+        product_a(1)
+        product_b(3)
+        look(0)
+        pick(2)
+        larger(1)
+        product_a(2)
+        look(1)
+        pick(3)
+        larger(2)
+        product_a(3)
+        look(2)
+        look(3)
+        larger(3)
 
         hid = tile("hid", PACK * O, BF16)
-        nc.vector.tensor_tensor(
-            hid[:].rearrange("p (c i t) -> p c t i", t=PACK, i=4),
-            top[:].rearrange("p (t c i) -> p c t i", t=PACK, i=4),
-            gate[:].rearrange("p (t c i) -> p c t i", t=PACK, i=4),
-            ALU.mult,
-        )
         hq = tile("hq", O, U32)
         hq_plane = tile("hq_plane", O, U8)
-        nc.vector.quantize_mx(hq[:].bitcast(E4M3), hq_plane[:], hid[:])
+        hid_v = hid[:].rearrange("p (c i t) -> p c t i", t=PACK, i=4)
+        top_v = top[:].rearrange("p (t c i) -> p c t i", t=PACK, i=4)
+        gate_v = gate[:].rearrange("p (t c i) -> p c t i", t=PACK, i=4)
+        half = O // 2
+        for u in range(2):
+            runs = slice(u * half // 4, (u + 1) * half // 4)
+            nc.vector.tensor_tensor(hid_v[:, runs], top_v[:, runs], gate_v[:, runs], ALU.mult)
+        for u in range(2):
+            places = slice(u * half, (u + 1) * half)
+            nc.vector.quantize_mx(
+                hq[:, places].bitcast(E4M3), hq_plane[:, places], hid[:, PACK * u * half : PACK * (u + 1) * half]
+            )
 
         for h in range(N // P):
-            y_ps = psum.tile([P, J], F32, name="acc")
+            y_ps = psum.tile([P, J], F32, name="bank_a%d" % (2 + h))
             words = slice(2 * h * P, 2 * (h + 1) * P)
-            cols = slice(h * P, (h + 1) * P)
+            ycols = slice(h * P, (h + 1) * P)
             nc.tensor.matmul_mx(
-                y_ps[:, 0:O], lhsT=ws[:, words].bitcast(E2M1), lhsT_scale=ws_plane[:, cols],
+                y_ps[:, 0:O], lhsT=ws[:, words].bitcast(E2M1), lhsT_scale=ws_plane[:, ycols],
                 rhs=sx.bitcast(E4M3), rhs_scale=sx_plane, start=True, stop=False,
             )
             nc.tensor.matmul_mx(
-                y_ps[:, 0:O], lhsT=wb[:, words].bitcast(E2M1), lhsT_scale=wb_plane[:, cols],
+                y_ps[:, 0:O], lhsT=wb[:, words].bitcast(E2M1), lhsT_scale=wb_plane[:, ycols],
                 rhs=hq[:].bitcast(E4M3), rhs_scale=hq_plane[:], start=False, stop=True,
             )
             y = tile("y%d" % h, O, F32)
             if h == 0:
                 nc.vector.tensor_copy(y[:], y_ps[:, 0:O])
-                nc.sync.dma_start(out[cols, :], y[:])
+                nc.sync.dma_start(out[ycols, :], y[:])
             else:
                 nc.scalar.copy(y[:], y_ps[:, 0:O])
-                nc.scalar.dma_start(out[cols, :], y[:])
+                nc.scalar.dma_start(out[ycols, :], y[:])

@@ -19,9 +19,14 @@ ALU = mybir.AluOpType
 
 P = 128
 PACK = 4
+GROUP = 16
 ROWS = 16
 QUAD = 32
-TOP = P - ROWS
+QUADS = P // QUAD
+QUAD_ROWS = ROWS // QUADS
+STAGE = P - ROWS
+LINE = 16
+HALVES = 2
 
 
 def tile_list_twow_agree_skip_plain_kernel(
@@ -33,19 +38,28 @@ def tile_list_twow_agree_skip_plain_kernel(
         sb = ctx.enter_context(tc.tile_pool(name="sb", bufs=1))
         psum = ctx.enter_context(tc.psum_pool(name="psum", bufs=1))
 
-        def tile(name, cols, dtype):
-            return sb.tile([P, cols], dtype, name=name, align_bytes=64)
+        def tile(name, width, dtype):
+            return sb.tile([P, width], dtype, name=name, align_bytes=64)
 
-        idx = tile("idx", J // 16, U16)
-        idx2 = tile("idx2", O // 16, U16)
-        idx3 = tile("idx3", O // 16, U16)
+        def fp8_words(words):
+            return words[0].rearrange("p n t -> p (n t)").bitcast(I32)
+
+        def part(i):
+            return slice(i * P, (i + 1) * P)
+
+        def fp4_part(i):
+            return slice(2 * i * P, 2 * (i + 1) * P)
+
+        idx = tile("idx", J // GROUP, U16)
+        idx2 = tile("idx2", O // GROUP, U16)
+        idx3 = tile("idx3", O // GROUP, U16)
         xt = tile("xt", T, U32)
         xt_rows = tile("xt_rows", T, U8)
         w2_rows = tile("w2_rows", R, U8)
         w_plane = tile("w_plane", R, U8)
-        rows = tile("rows", 2 * R + J, U8)
+        staged = tile("staged", 2 * R + J, U8)
         planes = tile("planes", 2 * R + J, U8)
-        xg_plane = planes[:, 2 * R :]
+        w_plane_given, w2_plane, xg_plane = planes[:, 0:R], planes[:, R : 2 * R], planes[:, 2 * R :]
         w_raw = tile("w_raw", 2 * R, U8)
         w2_raw = tile("w2_raw", R, U32)
         w_dealt = tile("w_dealt", 2 * R, U8)
@@ -54,80 +68,81 @@ def tile_list_twow_agree_skip_plain_kernel(
         xg_rows = tile("xg_rows", J, U8)
         slope = tile("slope", PACK, F32)
 
-        nc.vector.memset(xt_rows[0:TOP, :].bitcast(I32), 0)
-        nc.vector.memset(w2_rows[0:TOP, :].bitcast(I32), 0)
+        nc.vector.memset(xt_rows[0:STAGE, :].bitcast(I32), 0)
+        nc.vector.memset(w2_rows[0:STAGE, :].bitcast(I32), 0)
         nc.vector.memset(planes[:].bitcast(I32), 0)
 
         nc.sync.dma_start(idx[:], offs)
-        nc.scalar.dma_start(xt_rows[TOP:P, :].bitcast(I32), xt_scales[0].bitcast(I32))
-        nc.sync.dma_start(w2_rows[TOP:P, :].bitcast(I32), w2_scales[0].bitcast(I32))
-        nc.scalar.dma_start(rows[TOP:P, 0:R].bitcast(I32), w_scales[0].bitcast(I32))
+        nc.scalar.dma_start(xt_rows[STAGE:P, :].bitcast(I32), xt_scales[0].bitcast(I32))
+        nc.sync.dma_start(w2_rows[STAGE:P, :].bitcast(I32), w2_scales[0].bitcast(I32))
+        nc.scalar.dma_start(staged[STAGE:P, 0:R].bitcast(I32), w_scales[0].bitcast(I32))
         nc.sync.dma_start(idx3[:], offs3)
-        nc.sync.dma_start(xt[:].bitcast(I32), xt_words[0].rearrange("p n t -> p (n t)").bitcast(I32))
-        nc.sync.dma_start(w2_raw[:].bitcast(I32), w2_words[0].rearrange("p n t -> p (n t)").bitcast(I32))
+        nc.sync.dma_start(xt[:].bitcast(I32), fp8_words(xt_words))
+        nc.sync.dma_start(w2_raw[:].bitcast(I32), fp8_words(w2_words))
         nc.sync.dma_start(w_raw[:].bitcast(I32), w_words[0].bitcast(I32))
         nc.sync.dma_start(idx2[:], offs2)
+
         warm_in = tile("warm_in", 1, F32)
         warm_out = tile("warm_out", 1, F32)
         nc.vector.memset(warm_in[:], 0.0)
         nc.scalar.activation(warm_out[:], warm_in[:], ACT.Sigmoid)
-        nc.gpsimd.dma_start(slope[:], sg.rearrange("(p t) o -> p (t o)", t=PACK))
 
-        def spread(plane, source):
-            for q in range(4):
-                queue = nc.sync if q % 2 == 0 else nc.scalar
-                queue.dma_start(
-                    plane[QUAD * q : QUAD * q + 4, :].bitcast(I32),
-                    source[TOP + 4 * q : TOP + 4 * q + 4, :].bitcast(I32),
-                )
+        nc.gpsimd.dma_start(slope[:], sg.rearrange("(p t) o -> p (t o)", t=PACK))
 
         nc.vector.tensor_copy(xg_rows[:], xt_rows[:].indirect(idx[:]))
         nc.vector.tensor_copy(
-            rows[:, R : 2 * R].rearrange("p (t m) -> p t m", t=PACK), w2_rows[:].rearrange("p (m t) -> p t m", t=PACK)
+            staged[:, R : 2 * R].rearrange("p (t m) -> p t m", t=PACK),
+            w2_rows[:].rearrange("p (m t) -> p t m", t=PACK),
         )
-        nc.vector.tensor_copy(rows[:, 2 * R :].bitcast(I32), xg_rows[:].bitcast(I32))
-        spread(planes, rows)
+        nc.vector.tensor_copy(staged[:, 2 * R :].bitcast(I32), xg_rows[:].bitcast(I32))
+        for q in range(QUADS):
+            queue = nc.sync if q % 2 == 0 else nc.scalar
+            queue.dma_start(
+                planes[QUAD * q : QUAD * q + QUAD_ROWS, :].bitcast(I32),
+                staged[STAGE + QUAD_ROWS * q : STAGE + QUAD_ROWS * (q + 1), :].bitcast(I32),
+            )
+
         nc.vector.tensor_copy(xg[:], xt[:].indirect(idx[:]))
         nc.vector.tensor_copy(
-            w2_dealt[:].rearrange("p (t c i) -> p c t i", t=PACK, i=4),
-            w2_raw[:].rearrange("p (c i t) -> p c t i", t=PACK, i=4),
+            w2_dealt[:].rearrange("p (t c i) -> p c t i", t=PACK, i=LINE // 4),
+            w2_raw[:].rearrange("p (c i t) -> p c t i", t=PACK, i=LINE // 4),
         )
         nc.scalar.copy(
-            w_dealt[:].bitcast(U16).rearrange("p (t c i) -> p c t i", t=PACK, i=8),
-            w_raw[:].bitcast(U16).rearrange("p (c i t) -> p c t i", t=PACK, i=8),
+            w_dealt[:].bitcast(U16).rearrange("p (t c i) -> p c t i", t=PACK, i=LINE // 2),
+            w_raw[:].bitcast(U16).rearrange("p (c i t) -> p c t i", t=PACK, i=LINE // 2),
+        )
+        nc.vector.tensor_copy(
+            w_plane[:].rearrange("p (t m) -> p t m", t=PACK),
+            w_plane_given.rearrange("p (m t) -> p t m", t=PACK),
         )
 
-        nc.vector.tensor_copy(
-            w_plane[:].rearrange("p (t m) -> p t m", t=PACK), planes[:, 0:R].rearrange("p (m t) -> p t m", t=PACK)
-        )
         wb = w_raw[:, 0 : 2 * N]
         ws = w_raw[:, 2 * N : 4 * N]
         sx = w2_raw[:, 0:O]
-        spare = w2_raw[:, O:R].bitcast(U8)
-        wb_plane = spare[:, 0:N]
-        ws_plane = spare[:, N : 2 * N]
-        sx_plane = spare[:, 2 * N : 2 * N + O]
-        nc.sync.dma_start(sx.bitcast(I32), sx_words[0].rearrange("p n t -> p (n t)").bitcast(I32))
+        behind_sx = w2_raw[:, O:R].bitcast(U8)
+        wb_plane = behind_sx[:, 0:N]
+        ws_plane = behind_sx[:, N : 2 * N]
+        sx_plane = behind_sx[:, 2 * N : 2 * N + O]
+        nc.sync.dma_start(sx.bitcast(I32), fp8_words(sx_words))
         nc.sync.dma_start(ws.bitcast(I32), ws_words[0].bitcast(I32))
         nc.sync.dma_start(wb.bitcast(I32), wb_words[0].bitcast(I32))
         for plane, scales in ((sx_plane, sx_scales), (ws_plane, ws_scales), (wb_plane, wb_scales)):
-            for r in range(4):
-                nc.sync.dma_start(plane[r:P:QUAD, :].bitcast(I32), scales[0][r:ROWS:4, :].bitcast(I32))
+            for row in range(QUAD_ROWS):
+                nc.sync.dma_start(
+                    plane[row:P:QUAD, :].bitcast(I32), scales[0][row:ROWS:QUAD_ROWS, :].bitcast(I32)
+                )
 
         top = tile("top", PACK * O, F32)
         gate = tile("gate", PACK * O, F32)
         a = [tile("a%d" % t, J, F32) for t in range(PACK)]
         b = [tile("b%d" % t, J, F32) for t in range(PACK)]
-        b2 = tile("by2", PACK * O, F32)
-        b3 = tile("by3", PACK * O, F32)
-
-        def cols(t):
-            return slice(t * P, (t + 1) * P)
+        b_idx2 = tile("b_idx2", PACK * O, F32)
+        b_idx3 = tile("b_idx3", PACK * O, F32)
 
         def product_a(t):
             acc = psum.tile([P, J], F32, name="bank_a%d" % t)
             nc.tensor.matmul_mx(
-                acc[:], lhsT=w_dealt[:, 2 * t * P : 2 * (t + 1) * P].bitcast(E2M1), lhsT_scale=w_plane[:, cols(t)],
+                acc[:], lhsT=w_dealt[:, fp4_part(t)].bitcast(E2M1), lhsT_scale=w_plane[:, part(t)],
                 rhs=xg[:].bitcast(E5M2), rhs_scale=xg_plane, start=True, stop=True,
             )
             nc.scalar.copy(a[t][:], acc[:])
@@ -135,7 +150,7 @@ def tile_list_twow_agree_skip_plain_kernel(
         def product_b(t):
             acc = psum.tile([P, J], F32, name="bank_b%d" % t)
             nc.tensor.matmul_mx(
-                acc[:], lhsT=w2_dealt[:, cols(t)].bitcast(E4M3), lhsT_scale=planes[:, R + t * P : R + (t + 1) * P],
+                acc[:], lhsT=w2_dealt[:, part(t)].bitcast(E4M3), lhsT_scale=w2_plane[:, part(t)],
                 rhs=xg[:].bitcast(E5M2), rhs_scale=xg_plane, start=True, stop=True,
             )
             if t == 0:
@@ -144,68 +159,63 @@ def tile_list_twow_agree_skip_plain_kernel(
                 nc.scalar.copy(b[t][:], acc[:])
 
         def look(t):
-            nc.scalar.activation(gate[:, cols(t)], a[t][:].indirect(idx3[:]), ACT.Sigmoid, scale=slope[:, t : t + 1])
+            nc.scalar.activation(gate[:, part(t)], a[t][:].indirect(idx3[:]), ACT.Sigmoid, scale=slope[:, t : t + 1])
 
         def pick(t):
-            nc.vector.tensor_copy(b2[:, cols(t)], b[t][:].indirect(idx2[:]))
-            nc.vector.tensor_copy(b3[:, cols(t)], b[t][:].indirect(idx3[:]))
+            nc.vector.tensor_copy(b_idx2[:, part(t)], b[t][:].indirect(idx2[:]))
+            if t == 0:
+                nc.scalar.activation(b_idx3[:, part(t)], b[t][:].indirect(idx3[:]), ACT.Copy)
+            else:
+                nc.vector.tensor_copy(b_idx3[:, part(t)], b[t][:].indirect(idx3[:]))
 
         def larger(t):
-            nc.vector.tensor_tensor(top[:, cols(t)], b2[:, cols(t)], b3[:, cols(t)], ALU.max)
+            nc.vector.tensor_tensor(top[:, part(t)], b_idx2[:, part(t)], b_idx3[:, part(t)], ALU.max)
 
         product_b(0)
-        product_b(1)
-        pick(0)
-        product_a(0)
-        product_b(2)
-        pick(1)
-        larger(0)
-        product_a(1)
-        product_b(3)
-        look(0)
-        pick(2)
-        larger(1)
-        product_a(2)
-        look(1)
-        pick(3)
-        larger(2)
-        product_a(3)
-        look(2)
-        look(3)
-        larger(3)
+        for t in range(PACK):
+            if t + 1 < PACK:
+                product_b(t + 1)
+            if t >= 2:
+                look(t - 2)
+            pick(t)
+            if t >= 1:
+                larger(t - 1)
+            product_a(t)
+        look(PACK - 2)
+        look(PACK - 1)
+        larger(PACK - 1)
 
         hid = tile("hid", PACK * O, BF16)
         hq = tile("hq", O, U32)
         hq_plane = tile("hq_plane", O, U8)
-        hid_v = hid[:].rearrange("p (c i t) -> p c t i", t=PACK, i=4)
-        top_v = top[:].rearrange("p (t c i) -> p c t i", t=PACK, i=4)
-        gate_v = gate[:].rearrange("p (t c i) -> p c t i", t=PACK, i=4)
-        half = O // 2
-        for u in range(2):
-            runs = slice(u * half // 4, (u + 1) * half // 4)
-            nc.vector.tensor_tensor(hid_v[:, runs], top_v[:, runs], gate_v[:, runs], ALU.mult)
-        for u in range(2):
+        run = LINE // 4
+        hid_runs = hid[:].rearrange("p (c i t) -> p c t i", t=PACK, i=run)
+        top_runs = top[:].rearrange("p (t c i) -> p c t i", t=PACK, i=run)
+        gate_runs = gate[:].rearrange("p (t c i) -> p c t i", t=PACK, i=run)
+        half = O // HALVES
+        for u in range(HALVES):
+            runs = slice(u * half // run, (u + 1) * half // run)
+            nc.vector.tensor_tensor(hid_runs[:, runs], top_runs[:, runs], gate_runs[:, runs], ALU.mult)
+        for u in range(HALVES):
             places = slice(u * half, (u + 1) * half)
             nc.vector.quantize_mx(
                 hq[:, places].bitcast(E4M3), hq_plane[:, places], hid[:, PACK * u * half : PACK * (u + 1) * half]
             )
 
         for h in range(N // P):
-            y_ps = psum.tile([P, J], F32, name="bank_a%d" % (2 + h))
-            words = slice(2 * h * P, 2 * (h + 1) * P)
-            ycols = slice(h * P, (h + 1) * P)
+            acc = psum.tile([P, J], F32, name="bank_a%d" % (PACK - N // P + h))
             nc.tensor.matmul_mx(
-                y_ps[:, 0:O], lhsT=ws[:, words].bitcast(E2M1), lhsT_scale=ws_plane[:, ycols],
+                acc[:, 0:O], lhsT=ws[:, fp4_part(h)].bitcast(E2M1), lhsT_scale=ws_plane[:, part(h)],
                 rhs=sx.bitcast(E4M3), rhs_scale=sx_plane, start=True, stop=False,
             )
             nc.tensor.matmul_mx(
-                y_ps[:, 0:O], lhsT=wb[:, words].bitcast(E2M1), lhsT_scale=wb_plane[:, ycols],
+                acc[:, 0:O], lhsT=wb[:, fp4_part(h)].bitcast(E2M1), lhsT_scale=wb_plane[:, part(h)],
                 rhs=hq[:].bitcast(E4M3), rhs_scale=hq_plane[:], start=False, stop=True,
             )
             y = tile("y%d" % h, O, F32)
             if h == 0:
-                nc.vector.tensor_copy(y[:], y_ps[:, 0:O])
-                nc.sync.dma_start(out[ycols, :], y[:])
+                nc.vector.tensor_copy(y[:], acc[:, 0:O])
+                nc.sync.dma_start(out[part(h), :], y[:])
             else:
-                nc.scalar.copy(y[:], y_ps[:, 0:O])
-                nc.scalar.dma_start(out[ycols, :], y[:])
+                nc.scalar.copy(y[:], acc[:, 0:O])
+                nc.scalar.dma_start(out[part(h), :], y[:])

from contextlib import ExitStack

import concourse.mybir as mybir

K, T, J, R, O, N, L = 512, 1024, 256, 512, 128, 256, 512
FLOPS = 2 * (2 * K * R * J + R * N * O + L * N * O)

F32 = mybir.dt.float32
BF16 = mybir.dt.bfloat16
I32 = mybir.dt.int32
U32 = mybir.dt.uint32
U16 = mybir.dt.uint16
U8 = mybir.dt.uint8
E4M3 = mybir.dt.float8_e4m3fn_x4
E5M2 = mybir.dt.float8_e5m2_x4
E2M1 = mybir.dt.float4_e2m1fn_x4
ACT = mybir.ActivationFunctionType
ALU = mybir.AluOpType

P = 128
PACK = 4
GROUP = 16
ROWS = 16
QUAD = 32
QUADS = P // QUAD
QUAD_ROWS = ROWS // QUADS
STAGE = P - ROWS
LINE = 16
HALVES = 2


def tile_list_twow_agree_skip_plain_kernel(
    tc, xt_words, xt_scales, w_words, w_scales, w2_words, w2_scales, sg,
    wb_words, wb_scales, sx_words, sx_scales, ws_words, ws_scales, offs, offs2, offs3, out,
):
    nc = tc.nc
    with ExitStack() as ctx:
        sb = ctx.enter_context(tc.tile_pool(name="sb", bufs=1))
        psum = ctx.enter_context(tc.psum_pool(name="psum", bufs=1))

        def tile(name, width, dtype):
            return sb.tile([P, width], dtype, name=name, align_bytes=64)

        def fp8_words(words):
            return words[0].rearrange("p n t -> p (n t)").bitcast(I32)

        def part(i):
            return slice(i * P, (i + 1) * P)

        def fp4_part(i):
            return slice(2 * i * P, 2 * (i + 1) * P)

        idx = tile("idx", J // GROUP, U16)
        idx2 = tile("idx2", O // GROUP, U16)
        idx3 = tile("idx3", O // GROUP, U16)
        xt = tile("xt", T, U32)
        xt_rows = tile("xt_rows", T, U8)
        w2_rows = tile("w2_rows", R, U8)
        w_plane = tile("w_plane", R, U8)
        staged = tile("staged", 2 * R + J, U8)
        planes = tile("planes", 2 * R + J, U8)
        w_plane_given, w2_plane, xg_plane = planes[:, 0:R], planes[:, R : 2 * R], planes[:, 2 * R :]
        w_raw = tile("w_raw", 2 * R, U8)
        w2_raw = tile("w2_raw", R, U32)
        w_dealt = tile("w_dealt", 2 * R, U8)
        w2_dealt = tile("w2_dealt", R, U32)
        xg = tile("xg", J, U32)
        xg_rows = tile("xg_rows", J, U8)
        slope = tile("slope", PACK, F32)

        nc.vector.memset(xt_rows[0:STAGE, :].bitcast(I32), 0)
        nc.vector.memset(w2_rows[0:STAGE, :].bitcast(I32), 0)
        nc.vector.memset(planes[:].bitcast(I32), 0)

        nc.sync.dma_start(idx[:], offs)
        nc.scalar.dma_start(xt_rows[STAGE:P, :].bitcast(I32), xt_scales[0].bitcast(I32))
        nc.sync.dma_start(w2_rows[STAGE:P, :].bitcast(I32), w2_scales[0].bitcast(I32))
        nc.scalar.dma_start(staged[STAGE:P, 0:R].bitcast(I32), w_scales[0].bitcast(I32))
        nc.sync.dma_start(idx3[:], offs3)
        nc.sync.dma_start(xt[:].bitcast(I32), fp8_words(xt_words))
        nc.sync.dma_start(w2_raw[:].bitcast(I32), fp8_words(w2_words))
        nc.sync.dma_start(w_raw[:].bitcast(I32), w_words[0].bitcast(I32))
        nc.sync.dma_start(idx2[:], offs2)

        warm_in = tile("warm_in", 1, F32)
        warm_out = tile("warm_out", 1, F32)
        nc.vector.memset(warm_in[:], 0.0)
        nc.scalar.activation(warm_out[:], warm_in[:], ACT.Sigmoid)

        nc.gpsimd.dma_start(slope[:], sg.rearrange("(p t) o -> p (t o)", t=PACK))

        nc.vector.tensor_copy(xg_rows[:], xt_rows[:].indirect(idx[:]))
        nc.vector.tensor_copy(
            staged[:, R : 2 * R].rearrange("p (t m) -> p t m", t=PACK),
            w2_rows[:].rearrange("p (m t) -> p t m", t=PACK),
        )
        nc.vector.tensor_copy(staged[:, 2 * R :].bitcast(I32), xg_rows[:].bitcast(I32))
        for q in range(QUADS):
            queue = nc.sync if q % 2 == 0 else nc.scalar
            queue.dma_start(
                planes[QUAD * q : QUAD * q + QUAD_ROWS, :].bitcast(I32),
                staged[STAGE + QUAD_ROWS * q : STAGE + QUAD_ROWS * (q + 1), :].bitcast(I32),
            )

        nc.vector.tensor_copy(xg[:], xt[:].indirect(idx[:]))
        nc.vector.tensor_copy(
            w2_dealt[:].rearrange("p (t c i) -> p c t i", t=PACK, i=LINE // 4),
            w2_raw[:].rearrange("p (c i t) -> p c t i", t=PACK, i=LINE // 4),
        )
        nc.scalar.copy(
            w_dealt[:].bitcast(U16).rearrange("p (t c i) -> p c t i", t=PACK, i=LINE // 2),
            w_raw[:].bitcast(U16).rearrange("p (c i t) -> p c t i", t=PACK, i=LINE // 2),
        )
        nc.vector.tensor_copy(
            w_plane[:].rearrange("p (t m) -> p t m", t=PACK),
            w_plane_given.rearrange("p (m t) -> p t m", t=PACK),
        )

        wb = w_raw[:, 0 : 2 * N]
        ws = w_raw[:, 2 * N : 4 * N]
        sx = w2_raw[:, 0:O]
        behind_sx = w2_raw[:, O:R].bitcast(U8)
        wb_plane = behind_sx[:, 0:N]
        ws_plane = behind_sx[:, N : 2 * N]
        sx_plane = behind_sx[:, 2 * N : 2 * N + O]
        nc.sync.dma_start(sx.bitcast(I32), fp8_words(sx_words))
        nc.sync.dma_start(ws.bitcast(I32), ws_words[0].bitcast(I32))
        nc.sync.dma_start(wb.bitcast(I32), wb_words[0].bitcast(I32))
        for plane, scales in ((sx_plane, sx_scales), (ws_plane, ws_scales), (wb_plane, wb_scales)):
            for row in range(QUAD_ROWS):
                nc.sync.dma_start(
                    plane[row:P:QUAD, :].bitcast(I32), scales[0][row:ROWS:QUAD_ROWS, :].bitcast(I32)
                )

        top = tile("top", PACK * O, F32)
        gate = tile("gate", PACK * O, F32)
        a = [tile("a%d" % t, J, F32) for t in range(PACK)]
        b = [tile("b%d" % t, J, F32) for t in range(PACK)]
        b_idx2 = tile("b_idx2", PACK * O, F32)
        b_idx3 = tile("b_idx3", PACK * O, F32)

        def product_a(t):
            acc = psum.tile([P, J], F32, name="bank_a%d" % t)
            nc.tensor.matmul_mx(
                acc[:], lhsT=w_dealt[:, fp4_part(t)].bitcast(E2M1), lhsT_scale=w_plane[:, part(t)],
                rhs=xg[:].bitcast(E5M2), rhs_scale=xg_plane, start=True, stop=True,
            )
            nc.scalar.copy(a[t][:], acc[:])

        def product_b(t):
            acc = psum.tile([P, J], F32, name="bank_b%d" % t)
            nc.tensor.matmul_mx(
                acc[:], lhsT=w2_dealt[:, part(t)].bitcast(E4M3), lhsT_scale=w2_plane[:, part(t)],
                rhs=xg[:].bitcast(E5M2), rhs_scale=xg_plane, start=True, stop=True,
            )
            if t == 0:
                nc.vector.tensor_copy(b[t][:], acc[:])
            else:
                nc.scalar.copy(b[t][:], acc[:])

        def look(t):
            nc.scalar.activation(gate[:, part(t)], a[t][:].indirect(idx3[:]), ACT.Sigmoid, scale=slope[:, t : t + 1])

        def pick(t):
            nc.vector.tensor_copy(b_idx2[:, part(t)], b[t][:].indirect(idx2[:]))
            if t == 0:
                nc.scalar.activation(b_idx3[:, part(t)], b[t][:].indirect(idx3[:]), ACT.Copy)
            else:
                nc.vector.tensor_copy(b_idx3[:, part(t)], b[t][:].indirect(idx3[:]))

        def larger(t):
            nc.vector.tensor_tensor(top[:, part(t)], b_idx2[:, part(t)], b_idx3[:, part(t)], ALU.max)

        product_b(0)
        for t in range(PACK):
            if t + 1 < PACK:
                product_b(t + 1)
            if t >= 2:
                look(t - 2)
            pick(t)
            if t >= 1:
                larger(t - 1)
            product_a(t)
        look(PACK - 2)
        look(PACK - 1)
        larger(PACK - 1)

        hid = tile("hid", PACK * O, BF16)
        hq = tile("hq", O, U32)
        hq_plane = tile("hq_plane", O, U8)
        run = LINE // 4
        hid_runs = hid[:].rearrange("p (c i t) -> p c t i", t=PACK, i=run)
        top_runs = top[:].rearrange("p (t c i) -> p c t i", t=PACK, i=run)
        gate_runs = gate[:].rearrange("p (t c i) -> p c t i", t=PACK, i=run)
        half = O // HALVES
        for u in range(HALVES):
            runs = slice(u * half // run, (u + 1) * half // run)
            nc.vector.tensor_tensor(hid_runs[:, runs], top_runs[:, runs], gate_runs[:, runs], ALU.mult)
        for u in range(HALVES):
            places = slice(u * half, (u + 1) * half)
            nc.vector.quantize_mx(
                hq[:, places].bitcast(E4M3), hq_plane[:, places], hid[:, PACK * u * half : PACK * (u + 1) * half]
            )

        for h in range(N // P):
            acc = psum.tile([P, J], F32, name="bank_a%d" % (PACK - N // P + h))
            nc.tensor.matmul_mx(
                acc[:, 0:O], lhsT=ws[:, fp4_part(h)].bitcast(E2M1), lhsT_scale=ws_plane[:, part(h)],
                rhs=sx.bitcast(E4M3), rhs_scale=sx_plane, start=True, stop=False,
            )
            nc.tensor.matmul_mx(
                acc[:, 0:O], lhsT=wb[:, fp4_part(h)].bitcast(E2M1), lhsT_scale=wb_plane[:, part(h)],
                rhs=hq[:].bitcast(E4M3), rhs_scale=hq_plane[:], start=False, stop=True,
            )
            y = tile("y%d" % h, O, F32)
            if h == 0:
                nc.vector.tensor_copy(y[:], acc[:, 0:O])
                nc.sync.dma_start(out[part(h), :], y[:])
            else:
                nc.scalar.copy(y[:], acc[:, 0:O])
                nc.scalar.dma_start(out[part(h), :], y[:])
